import numpy as np, ml_dtypes
CORES = [0,16,32,48,64,80,96,112,128,144,160,176,192,208,224,240]
N = 16
GROUPS = [[0,1,2,3,4,5,6,7],[8,9,10,11,12,13,14,15]]
def setup_inputs(rng):
    return {"x": rng.standard_normal((N, 128, 8), dtype=np.float32).astype(ml_dtypes.bfloat16)}
def reference(x):
    y = np.empty((N, 128, 8), x.dtype)
    for g in GROUPS:
        n = len(g); b = x.shape[2] // n
        for i, r in enumerate(g):
            y[r] = np.concatenate([x[s][:, i * b:(i + 1) * b] for s in g], axis=1)
    return {"y": y}

from concourse.bass import DstId, RemoteDMATransfer

SCRATCH = {
    "xs": ("sbuf", [128, 8], "bfloat16"),
    "land": ("sbuf", [128, 8], "bfloat16"),
}
SEMAPHORES = ["loaded", "sent", "ready", "stored"]

OFF_CHIP_ENGINES = 8


def rank_program(g, core, T, topo):
    rank = T.rank_of(core)
    if rank is None:
        return

    group = [grp for grp in T.tables["GROUPS"] if rank in grp][0]
    n = len(group)
    i = group.index(rank)
    b = T.x.shape[1] // n

    def blk(t, k):
        return t[:, k * b:(k + 1) * b]

    g.sync.dma_start(T.xs[:], T.x[:]).then_inc(T.sem.loaded, 16)

    g.scalar.wait_ge(T.sem.loaded, 16)
    g.scalar.dma_start(blk(T.land, i), blk(T.xs, i)).then_inc(T.sem.ready, 16)

    g.wait_ge(T.sem.loaded, 16)
    peers = [j for j in range(n) if j != i]
    for lo in range(0, len(peers), OFF_CHIP_ENGINES):
        transfers = []
        for e, j in enumerate(peers[lo:lo + OFF_CHIP_ENGINES]):
            rid, pid = topo.addr(T.cores[group[j]], core)
            transfers.append(RemoteDMATransfer(
                dst_ids=[DstId(rid=rid, pnc=pid)],
                dma_engine_mask=1 << e,
                remote_sem=T.sem.ready,
                src=blk(T.xs, j),
                dst=blk(T.land, i),
            ))
        g.remote_dma_fused(transfers, local_sem=T.sem.sent)
    g.wait_ge(T.sem.sent, n - 1)

    g.sync.wait_ge(T.sem.ready, (n - 1) + 16)
    g.sync.dma_start(T.y[:], T.land[:]).then_inc(T.sem.stored, 16)
    g.sync.wait_ge(T.sem.stored, 16)
